import numpy as np
import ml_dtypes


def mxq(x, axis, fmt="e4m3"):
    dtype, down = {"e4m3": (ml_dtypes.float8_e4m3fn, 7), "e5m2": (ml_dtypes.float8_e5m2, 14)}[fmt]
    v = np.moveaxis(np.asarray(x, np.float32).astype(ml_dtypes.bfloat16).astype(np.float64), axis, -1)
    blocks = v.reshape(v.shape[:-1] + (-1, 32))
    amax = np.abs(blocks).max(-1, keepdims=True)
    byte = np.maximum(np.where(amax > 0, np.frexp(amax)[1] - 1 + 127, 0) - down, 1)
    scale = np.exp2(byte - 127.0)
    codes = (blocks / scale).astype(np.float32).astype(dtype).astype(np.float64)
    return np.moveaxis((codes * scale).reshape(v.shape), -1, axis)


WIDE = False


def mx_kscale(k):
    if not WIDE:
        return np.ones(k)
    levels = np.array([10, -10, 5, -5, 0])
    if k % 512:
        return np.exp2(np.random.permutation(np.resize(levels, k // 32))).repeat(32)
    a = np.empty((k // 512, 16))
    for p in range(k // 512):
        a[p, :8] = np.random.permutation(np.resize(levels, 8))
        for g in range(8):
            far = levels[np.abs(levels - a[p, g]) >= 10]
            a[p, g + 8] = far[np.random.randint(len(far))]
    return np.exp2(a.ravel()).repeat(32)


def f64(x):
    return np.asarray(x).astype(np.float64)


def striped(idx):
    return np.tile(idx.reshape(-1, 16).T, (8, 1)).astype(np.uint16)


def unstriped(offs):
    return offs[:16].T.reshape(-1).astype(np.int64)


def relu(v):
    return np.maximum(v, 0.0)


K, T, D, V, H, N = 1536, 512, 6, 256, 512, 256
P = 2 ** 7


def setup_inputs():
    n = np.random.standard_normal
    s = mx_kscale(K)[:, None]
    u = mx_kscale(H)
    return {
        "xT": (n((K, T)) * s).astype(np.float32),
        "w1": (n((K, H)) / np.sqrt(K) / s * u).astype(np.float32),
        "w2": (n((H, N)) / np.sqrt(H) / u[:, None]).astype(np.float32),
        "gate": np.tile(np.random.uniform(0.2, 1.0, (D, 1, V)) / np.sqrt(D), (1, P, 1)).astype(np.float32),
        "pos1": striped(np.random.permutation(T)[:V]),
        "pos2": striped(np.random.permutation(T)[:V]),
        "pos3": striped(np.random.permutation(T)[:V]),
        "pos4": striped(np.random.permutation(T)[:V]),
        "pos5": striped(np.random.permutation(T)[:V]),
        "pos6": striped(np.random.permutation(T)[:V]),
    }


def reference(xT, w1, w2, gate, pos1, pos2, pos3, pos4, pos5, pos6):
    h = relu(mxq(f64(w1), 0, "e4m3").T @ mxq(f64(xT), 0, "e4m3"))
    z = sum(f64(gate)[d, :1] * h[:, unstriped(p)] for d, p in enumerate((pos1, pos2, pos3, pos4, pos5, pos6)))
    return mxq(f64(w2), 0, "e4m3").T @ mxq(z, 0, "e4m3")

@@ -1,0 +1,230 @@
+from contextlib import ExitStack
+
+import concourse.mybir as mybir
+from concourse.masks import make_identity
+
+K, T, D, V, H, N = 1536, 512, 6, 256, 512, 256
+FLOPS = 2 * K * H * T + 2 * H * N * V
+
+F32 = mybir.dt.float32
+BF16 = mybir.dt.bfloat16
+U32 = mybir.dt.uint32
+U16 = mybir.dt.uint16
+U8 = mybir.dt.uint8
+FP8X4 = mybir.dt.float8_e4m3fn_x4
+RELU = mybir.ActivationFunctionType.Relu
+MULT = mybir.AluOpType.mult
+
+P = 128
+J = 4
+KP = P * J
+PASSES = K // KP
+CB = H // P
+VH = V // P
+
+
+def interleave(copy, grouped, raw):
+    copy(
+        out=grouped.rearrange("p (c i) j -> p c j i", i=4),
+        in_=raw.rearrange("p j (c i) -> p c j i", i=4),
+    )
+
+
+def quantize(nc, codes, scales, grouped):
+    nc.vector.quantize_mx(
+        out=codes.bitcast(FP8X4), scales=scales, in_=grouped.rearrange("p c j -> p (c j)")
+    )
+
+
+def tile_picked_gcn_mlp_relu_sub_l_kernel(
+    tc, xT, w1, w2, gate, pos1, pos2, pos3, pos4, pos5, pos6, out
+):
+    nc = tc.nc
+    with ExitStack() as ctx:
+        keep = ctx.enter_context(tc.tile_pool(name="keep", bufs=1))
+        prods = ctx.enter_context(tc.tile_pool(name="prods", bufs=4))
+        psum_h = ctx.enter_context(tc.psum_pool(name="psum_h", bufs=2))
+        psum_z = ctx.enter_context(tc.psum_pool(name="psum_z", bufs=4))
+        psum_m = ctx.enter_context(tc.psum_pool(name="psum_m", bufs=2))
+
+        gate_rows = keep.tile([P, V], F32)
+        nc.scalar.dma_start(out=gate_rows[:], in_=gate.rearrange("d r v -> (d r) v").rearrange("(p s) v -> p s v", s=D)[:, 0, :])
+
+        x_raw = []
+        for g in range(PASSES):
+            t = keep.tile([P, J, T], F32, name=f"x_raw{g}")
+            nc.sync.dma_start(out=t[:], in_=xT[g * KP : (g + 1) * KP, :].rearrange("(p j) t -> p j t", j=J))
+            x_raw.append(t)
+        w1_cols = [(0, 128), (128, 256), (256, 512)]
+        w1_raw = []
+
+        def load_w1(b):
+            lo, hi = w1_cols[b]
+            tiles = []
+            for g in range(PASSES):
+                t = keep.tile([P, J, hi - lo], F32, name=f"w1_raw{b}_{g}")
+                nc.sync.dma_start(out=t[:], in_=w1[g * KP : (g + 1) * KP, lo:hi].rearrange("(p j) c -> p j c", j=J))
+                tiles.append(t)
+            w1_raw.append(tiles)
+
+        load_w1(0)
+        lists = []
+        for d, pos in enumerate((pos1, pos2, pos3, pos4, pos5, pos6)):
+            t = keep.tile([P, V // 16], U16, name=f"list{d}")
+            nc.sync.dma_start(t[:], pos)
+            lists.append(t)
+        load_w1(1)
+        load_w1(2)
+        w2_raw = keep.tile([P, J, N], F32)
+        nc.sync.dma_start(out=w2_raw[:], in_=w2.rearrange("(p j) m -> p j m", j=J))
+
+        ident = keep.tile([P, P], F32)
+        make_identity(nc, ident[:])
+        gate_cols_ps = psum_m.tile([P, VH, P], F32, name="gate_cols_ps", tag="m")
+        gate_cols = keep.tile([P, VH, P], F32)
+        for c in range(VH):
+            nc.tensor.transpose(gate_cols_ps[:, c, :], gate_rows[:, c * P : (c + 1) * P], ident[:])
+        nc.scalar.copy(out=gate_cols[:], in_=gate_cols_ps[:])
+        gate_all = keep.tile([P, D, V], F32)
+        for d2 in range(D // 2):
+            gps = psum_m.tile([P, 2, V], F32, name="gate_ps", tag="m")
+            for e in range(2):
+                for c in range(VH):
+                    q = -(-P * (2 * d2 + e) // D)
+                    nc.tensor.transpose(
+                        gps[:, e, c * P : (c + 1) * P], gate_cols[:, c, q : q + 1].to_broadcast([P, P]), ident[:]
+                    )
+            nc.scalar.copy(out=gate_all[:, 2 * d2 : 2 * d2 + 2, :], in_=gps[:])
+
+        x_codes, x_scales = [], []
+        for g in range(PASSES):
+            codes = keep.tile([P, T], U32, align_bytes=64, name=f"x_codes{g}")
+            scales = keep.tile([P, T], U8, align_bytes=64, name=f"x_scales{g}")
+            for half, copy in enumerate((nc.vector.tensor_copy, nc.scalar.copy)):
+                cols = slice(half * 256, half * 256 + 256)
+                grouped = keep.tile([P, 256, J], BF16, align_bytes=64, name=f"x_grouped{g}_{half}")
+                interleave(copy, grouped[:], x_raw[g][:, :, cols])
+                quantize(nc, codes[:, cols], scales[:, cols], grouped[:])
+            x_codes.append(codes)
+            x_scales.append(scales)
+
+        def prepare_w1(c, copies):
+            b = min(c, 2)
+            off = c * P - w1_cols[b][0]
+            codes = keep.tile([P, PASSES, P], U32, align_bytes=64, name=f"w1_codes{c}")
+            scales = keep.tile([P, PASSES, P], U8, align_bytes=64, name=f"w1_scales{c}")
+            steps = []
+            for g in range(PASSES):
+                grouped = keep.tile([P, P, J], BF16, align_bytes=64, name=f"w1_grouped{c}_{g}")
+                interleave(copies[g], grouped[:], w1_raw[b][g][:, :, off : off + P])
+                steps.append(lambda g=g, grouped=grouped: quantize(nc, codes[:, g, :], scales[:, g, :], grouped[:]))
+            return codes, scales, steps
+
+        def project(c, codes, scales, widths):
+            h = keep.tile([P, T], F32, name=f"h{c}")
+            lo = 0
+            for i, n in enumerate(widths):
+                cols = slice(lo, lo + n)
+                hp = psum_h.tile([P, T], F32, name="hp", tag="hp")
+                for g in range(PASSES):
+                    nc.tensor.matmul_mx(
+                        out=hp[:, :n],
+                        lhsT=codes[:, g, :].bitcast(FP8X4),
+                        lhsT_scale=scales[:, g, :],
+                        rhs=x_codes[g][:, cols].bitcast(FP8X4),
+                        rhs_scale=x_scales[g][:, cols],
+                        start=(g == 0),
+                        stop=(g == PASSES - 1),
+                    )
+                if i == 0:
+                    nc.scalar.activation(out=h[:, cols], in_=hp[:, :n], func=RELU)
+                else:
+                    nc.vector.tensor_relu(out=h[:, cols], in_=hp[:, :n])
+                lo += n
+            return h
+
+        zt = []
+        for vh in range(VH):
+            t = keep.tile([P, 2, P, 2], BF16, align_bytes=64, name=f"zt{vh}")
+            zt.append(t)
+
+        def gather_sum(c, h, first, count, between):
+            zps = []
+            for vh in range(first, first + count):
+                t = psum_z.tile([P, P], F32, name="zps", tag="zps")
+                zps.append(t)
+            n = count * P
+            for d in range(D):
+                prod = prods.tile([P, V], F32, name="prod", tag="prod")
+                nc.vector.tensor_tensor(
+                    prod[:, :n],
+                    h[:].indirect(lists[d][:, first * 8 : (first + count) * 8]),
+                    gate_all[:, d, first * P : first * P + n],
+                    MULT,
+                )
+                for i in range(count):
+                    nc.tensor.matmul(
+                        zps[i][:], prod[:, i * P : (i + 1) * P], ident[:],
+                        start=(d == 0), stop=(d == D - 1), is_transpose=True,
+                    )
+                for step in between.get(d, ()):
+                    step()
+            for i in range(count):
+                nc.scalar.copy(
+                    out=zt[first + i][:, :, 32 * c : 32 * c + 32, :],
+                    in_=zps[i][:].rearrange("v (p u e) -> v u p e", u=2, e=2),
+                )
+
+        w2_grouped = keep.tile([P, N, J], BF16, align_bytes=64)
+        w2_codes = keep.tile([P, N], U32, align_bytes=64)
+        w2_scales = keep.tile([P, N], U8, align_bytes=64)
+        z_codes = keep.tile([P, V], U32, align_bytes=64)
+        z_scales = keep.tile([P, V], U8, align_bytes=64)
+        hs = {}
+
+        def finish(vh):
+            cols = slice(vh * P, (vh + 1) * P)
+            words = zt[vh][:].rearrange("v u p e -> v (u p e)").bitcast(F32)
+            back = psum_m.tile([P, 2, P], F32, name="back", tag="m")
+            for u in range(2):
+                nc.tensor.transpose(back[:, u, :], words[:, u * P : (u + 1) * P], ident[:])
+            grouped = keep.tile([P, P, J], BF16, align_bytes=64, name=f"z_grouped{vh}")
+            nc.vector.tensor_copy(
+                out=grouped[:].rearrange("p v j -> p (v j)").bitcast(F32).rearrange("p (v u) -> p v u", u=2),
+                in_=back[:].rearrange("p u v -> p v u"),
+            )
+            quantize(nc, z_codes[:, cols], z_scales[:, cols], grouped[:])
+            res = keep.tile([P, 2, P], F32, name=f"res{vh}")
+            ops = psum_h.tile([P, 2, P], F32, name="ops", tag="hp")
+            for mb in range(N // P):
+                nc.tensor.matmul_mx(
+                    out=ops[:, mb, :],
+                    lhsT=w2_codes[:, mb * P : (mb + 1) * P].bitcast(FP8X4),
+                    lhsT_scale=w2_scales[:, mb * P : (mb + 1) * P],
+                    rhs=z_codes[:, cols].bitcast(FP8X4),
+                    rhs_scale=z_scales[:, cols],
+                    start=True,
+                    stop=True,
+                )
+            nc.scalar.copy(out=res[:], in_=ops[:])
+            nc.sync.dma_start(out=out[:, cols].rearrange("(b p) v -> p b v", p=P), in_=res[:])
+
+        sc, ve = nc.scalar.copy, nc.vector.tensor_copy
+        codes, scales, steps = prepare_w1(0, (sc, sc, ve))
+        for step in steps:
+            step()
+        hs[0] = project(0, codes, scales, (256, 256))
+        for c in range(CB - 1):
+            codes, scales, steps = prepare_w1(c + 1, (sc, sc, sc))
+
+            def next_h(c=c, codes=codes, scales=scales):
+                hs[c + 1] = project(c + 1, codes, scales, (512,))
+
+            between = {1: steps[:1], 2: steps[1:2], 3: steps[2:] + [next_h]}
+            if c == CB - 2:
+                interleave(sc, w2_grouped[:], w2_raw[:])
+                between[5] = [lambda: quantize(nc, w2_codes[:], w2_scales[:], w2_grouped[:])]
+            gather_sum(c, hs[c], 0, VH, between)
+        gather_sum(CB - 1, hs[CB - 1], 0, 1, {})
+        gather_sum(CB - 1, hs[CB - 1], 1, 1, {3: [lambda: finish(0)]})
+        finish(1)

@@ -42,91 +42,83 @@ def tile_picked_gcn_mlp_relu_sub_l_kernel(
     nc = tc.nc
     with ExitStack() as ctx:
         keep = ctx.enter_context(tc.tile_pool(name="keep", bufs=1))
-        prods = ctx.enter_context(tc.tile_pool(name="prods", bufs=4))
+        prods = ctx.enter_context(tc.tile_pool(name="prods", bufs=12))
         psum_h = ctx.enter_context(tc.psum_pool(name="psum_h", bufs=2))
         psum_z = ctx.enter_context(tc.psum_pool(name="psum_z", bufs=4))
         psum_m = ctx.enter_context(tc.psum_pool(name="psum_m", bufs=2))
 
-        gate_rows = keep.tile([P, V], F32)
-        nc.scalar.dma_start(out=gate_rows[:], in_=gate.rearrange("d r v -> (d r) v").rearrange("(p s) v -> p s v", s=D)[:, 0, :])
+        gate_all = []
 
-        x_raw = []
-        for g in range(PASSES):
-            t = keep.tile([P, J, T], F32, name=f"x_raw{g}")
-            nc.sync.dma_start(out=t[:], in_=xT[g * KP : (g + 1) * KP, :].rearrange("(p j) t -> p j t", j=J))
-            x_raw.append(t)
-        w1_cols = [(0, 128), (128, 256), (256, 512)]
-        w1_raw = []
+        def load_gate():
+            first = D // 2 * len(gate_all)
+            t = keep.tile([P, D // 2, V], F32, name=f"gate{first}")
+            nc.sync.dma_start(out=t[:], in_=gate[first : first + D // 2].rearrange("d p v -> p d v"))
+            gate_all.append(t)
 
-        def load_w1(b):
-            lo, hi = w1_cols[b]
-            tiles = []
-            for g in range(PASSES):
-                t = keep.tile([P, J, hi - lo], F32, name=f"w1_raw{b}_{g}")
-                nc.sync.dma_start(out=t[:], in_=w1[g * KP : (g + 1) * KP, lo:hi].rearrange("(p j) c -> p j c", j=J))
-                tiles.append(t)
-            w1_raw.append(tiles)
+        w1_raw = [[], [], [], []]
 
-        load_w1(0)
+        def load_w1(b, g):
+            t = keep.tile([P, J, P], F32, name=f"w1_raw{b}_{g}")
+            nc.sync.dma_start(out=t[:], in_=w1[g * KP : (g + 1) * KP, b * P : (b + 1) * P].rearrange("(p j) c -> p j c", j=J))
+            w1_raw[b].append(t)
+
+        x_pieces = [(0, 0, T), (1, 0, T), (2, 0, T // 2), (2, T // 2, T)]
+        x_raw = {}
+
+        def load_x(g, lo, hi):
+            t = keep.tile([P, J, hi - lo], F32, name=f"x_raw{g}_{lo}")
+            nc.sync.dma_start(out=t[:], in_=xT[g * KP : (g + 1) * KP, lo:hi].rearrange("(p j) t -> p j t", j=J))
+            x_raw[g, lo] = t
+
         lists = []
-        for d, pos in enumerate((pos1, pos2, pos3, pos4, pos5, pos6)):
+
+        def load_list():
+            d = len(lists)
             t = keep.tile([P, V // 16], U16, name=f"list{d}")
-            nc.sync.dma_start(t[:], pos)
+            nc.sync.dma_start(t[:], (pos1, pos2, pos3, pos4, pos5, pos6)[d])
             lists.append(t)
-        load_w1(1)
-        load_w1(2)
+
+        for g in range(PASSES):
+            load_w1(0, g)
+        load_list()
+        for piece in x_pieces:
+            load_x(*piece)
+        load_gate()
+        for g in range(PASSES):
+            load_w1(1, g)
+        load_list()
+        load_list()
+        load_gate()
+        for d in range(3):
+            load_list()
+        for b in (2, 3):
+            for g in range(PASSES):
+                load_w1(b, g)
         w2_raw = keep.tile([P, J, N], F32)
         nc.sync.dma_start(out=w2_raw[:], in_=w2.rearrange("(p j) m -> p j m", j=J))
 
         ident = keep.tile([P, P], F32)
         make_identity(nc, ident[:])
-        gate_cols_ps = psum_m.tile([P, VH, P], F32, name="gate_cols_ps", tag="m")
-        gate_cols = keep.tile([P, VH, P], F32)
-        for c in range(VH):
-            nc.tensor.transpose(gate_cols_ps[:, c, :], gate_rows[:, c * P : (c + 1) * P], ident[:])
-        nc.scalar.copy(out=gate_cols[:], in_=gate_cols_ps[:])
-        gate_all = keep.tile([P, D, V], F32)
-        for d2 in range(D // 2):
-            gps = psum_m.tile([P, 2, V], F32, name="gate_ps", tag="m")
-            for e in range(2):
-                for c in range(VH):
-                    q = -(-P * (2 * d2 + e) // D)
-                    nc.tensor.transpose(
-                        gps[:, e, c * P : (c + 1) * P], gate_cols[:, c, q : q + 1].to_broadcast([P, P]), ident[:]
-                    )
-            nc.scalar.copy(out=gate_all[:, 2 * d2 : 2 * d2 + 2, :], in_=gps[:])
-
-        x_codes, x_scales = [], []
-        for g in range(PASSES):
-            codes = keep.tile([P, T], U32, align_bytes=64, name=f"x_codes{g}")
-            scales = keep.tile([P, T], U8, align_bytes=64, name=f"x_scales{g}")
-            for half, copy in enumerate((nc.vector.tensor_copy, nc.scalar.copy)):
-                cols = slice(half * 256, half * 256 + 256)
-                grouped = keep.tile([P, 256, J], BF16, align_bytes=64, name=f"x_grouped{g}_{half}")
-                interleave(copy, grouped[:], x_raw[g][:, :, cols])
-                quantize(nc, codes[:, cols], scales[:, cols], grouped[:])
-            x_codes.append(codes)
-            x_scales.append(scales)
 
         def prepare_w1(c, copies):
-            b = min(c, 2)
-            off = c * P - w1_cols[b][0]
             codes = keep.tile([P, PASSES, P], U32, align_bytes=64, name=f"w1_codes{c}")
             scales = keep.tile([P, PASSES, P], U8, align_bytes=64, name=f"w1_scales{c}")
             steps = []
             for g in range(PASSES):
                 grouped = keep.tile([P, P, J], BF16, align_bytes=64, name=f"w1_grouped{c}_{g}")
-                interleave(copies[g], grouped[:], w1_raw[b][g][:, :, off : off + P])
+                interleave(copies[g], grouped[:], w1_raw[c][g][:])
                 steps.append(lambda g=g, grouped=grouped: quantize(nc, codes[:, g, :], scales[:, g, :], grouped[:]))
             return codes, scales, steps
 
         def project(c, codes, scales, widths):
             h = keep.tile([P, T], F32, name=f"h{c}")
-            lo = 0
-            for i, n in enumerate(widths):
-                cols = slice(lo, lo + n)
+            parts, lo = [], 0
+            for n in widths:
                 hp = psum_h.tile([P, T], F32, name="hp", tag="hp")
-                for g in range(PASSES):
+                parts.append((hp, n, slice(lo, lo + n)))
+                lo += n
+            for g in range(PASSES):
+                for hp, n, cols in parts:
                     nc.tensor.matmul_mx(
                         out=hp[:, :n],
                         lhsT=codes[:, g, :].bitcast(FP8X4),
@@ -136,11 +128,11 @@ def tile_picked_gcn_mlp_relu_sub_l_kernel(
                         start=(g == 0),
                         stop=(g == PASSES - 1),
                     )
+            for i, (hp, n, cols) in enumerate(parts):
                 if i == 0:
                     nc.scalar.activation(out=h[:, cols], in_=hp[:, :n], func=RELU)
                 else:
                     nc.vector.tensor_relu(out=h[:, cols], in_=hp[:, :n])
-                lo += n
             return h
 
         zt = []
@@ -159,7 +151,7 @@ def tile_picked_gcn_mlp_relu_sub_l_kernel(
                 nc.vector.tensor_tensor(
                     prod[:, :n],
                     h[:].indirect(lists[d][:, first * 8 : (first + count) * 8]),
-                    gate_all[:, d, first * P : first * P + n],
+                    gate_all[d // 3][:, d % 3, first * P : first * P + n],
                     MULT,
                 )
                 for i in range(count):
@@ -209,22 +201,53 @@ def tile_picked_gcn_mlp_relu_sub_l_kernel(
             nc.scalar.copy(out=res[:], in_=ops[:])
             nc.sync.dma_start(out=out[:, cols].rearrange("(b p) v -> p b v", p=P), in_=res[:])
 
+        x_codes, x_scales = [], []
+        for g in range(PASSES):
+            t = keep.tile([P, T], U32, align_bytes=64, name=f"x_codes{g}")
+            x_codes.append(t)
+            t = keep.tile([P, T], U8, align_bytes=64, name=f"x_scales{g}")
+            x_scales.append(t)
+
+        def prepare_x(g, lo, hi, vector_cols):
+            width = hi - lo
+            grouped = keep.tile([P, width, J], BF16, align_bytes=64, name=f"x_grouped{g}_{lo}")
+            raw = x_raw[g, lo]
+            interleave(nc.vector.tensor_copy, grouped[:, :vector_cols, :], raw[:, :, :vector_cols])
+            interleave(nc.scalar.copy, grouped[:, vector_cols:, :], raw[:, :, vector_cols:])
+            for first, last in ((0, vector_cols), (vector_cols, width)) if width > 256 else ((0, width),):
+                cols = slice(lo + first, lo + last)
+                quantize(nc, x_codes[g][:, cols], x_scales[g][:, cols], grouped[:, first:last, :])
+
         sc, ve = nc.scalar.copy, nc.vector.tensor_copy
-        codes, scales, steps = prepare_w1(0, (sc, sc, ve))
-        for step in steps:
-            step()
-        hs[0] = project(0, codes, scales, (256, 256))
-        for c in range(CB - 1):
-            codes, scales, steps = prepare_w1(c + 1, (sc, sc, sc))
+        w1q = {}
 
-            def next_h(c=c, codes=codes, scales=scales):
-                hs[c + 1] = project(c + 1, codes, scales, (512,))
+        def prepare(c, copies):
+            w1q[c] = prepare_w1(c, copies)
 
-            between = {1: steps[:1], 2: steps[1:2], 3: steps[2:] + [next_h]}
-            if c == CB - 2:
+        def q(c, g):
+            w1q[c][2][g]()
+
+        def next_h(c, widths):
+            hs[c] = project(c, w1q[c][0], w1q[c][1], widths)
+
+        prepare(0, (ve, sc, ve))
+        for g in range(PASSES):
+            q(0, g)
+        for g, lo, hi in x_pieces:
+            prepare_x(g, lo, hi, 256 if hi - lo == T else 160)
+        next_h(0, (256, 256))
+        for c in range(CB):
+            if c + 1 < CB:
+                prepare(c + 1, (sc, sc, sc))
+                for g in range(PASSES):
+                    q(c + 1, g)
+                next_h(c + 1, (T,))
+            else:
                 interleave(sc, w2_grouped[:], w2_raw[:])
-                between[5] = [lambda: quantize(nc, w2_codes[:], w2_scales[:], w2_grouped[:])]
-            gather_sum(c, hs[c], 0, VH, between)
-        gather_sum(CB - 1, hs[CB - 1], 0, 1, {})
-        gather_sum(CB - 1, hs[CB - 1], 1, 1, {3: [lambda: finish(0)]})
+                quantize(nc, w2_codes[:], w2_scales[:], w2_grouped[:])
+            if c + 1 < CB:
+                gather_sum(c, hs[c], 0, VH, {})
+            else:
+                gather_sum(c, hs[c], 0, 1, {})
+                gather_sum(c, hs[c], 1, 1, {3: [lambda: finish(0)]})
         finish(1)

@@ -49,11 +49,11 @@ def tile_picked_gcn_mlp_relu_sub_l_kernel(
 
         gate_all = []
 
-        def load_gate():
-            first = D // 2 * len(gate_all)
-            t = keep.tile([P, D // 2, V], F32, name=f"gate{first}")
-            nc.sync.dma_start(out=t[:], in_=gate[first : first + D // 2].rearrange("d p v -> p d v"))
-            gate_all.append(t)
+        def load_gate(first, last):
+            t = keep.tile([P, last - first, V], F32, name=f"gate{first}")
+            nc.sync.dma_start(out=t[:], in_=gate[first:last].rearrange("d p v -> p d v"))
+            for i in range(last - first):
+                gate_all.append(t[:, i, :])
 
         w1_raw = [[], [], [], []]
 
@@ -62,13 +62,12 @@ def tile_picked_gcn_mlp_relu_sub_l_kernel(
             nc.sync.dma_start(out=t[:], in_=w1[g * KP : (g + 1) * KP, b * P : (b + 1) * P].rearrange("(p j) c -> p j c", j=J))
             w1_raw[b].append(t)
 
-        x_pieces = [(0, 0, T), (1, 0, T), (2, 0, T // 2), (2, T // 2, T)]
-        x_raw = {}
+        x_raw = []
 
-        def load_x(g, lo, hi):
-            t = keep.tile([P, J, hi - lo], F32, name=f"x_raw{g}_{lo}")
-            nc.sync.dma_start(out=t[:], in_=xT[g * KP : (g + 1) * KP, lo:hi].rearrange("(p j) t -> p j t", j=J))
-            x_raw[g, lo] = t
+        def load_x(g):
+            t = keep.tile([P, J, T], F32, name=f"x_raw{g}")
+            nc.sync.dma_start(out=t[:], in_=xT[g * KP : (g + 1) * KP, :].rearrange("(p j) t -> p j t", j=J))
+            x_raw.append(t)
 
         lists = []
 
@@ -81,16 +80,15 @@ def tile_picked_gcn_mlp_relu_sub_l_kernel(
         for g in range(PASSES):
             load_w1(0, g)
         load_list()
-        for piece in x_pieces:
-            load_x(*piece)
-        load_gate()
+        load_list()
+        for g in range(PASSES):
+            load_x(g)
+        for d in range(4):
+            load_list()
+        load_gate(0, 4)
         for g in range(PASSES):
             load_w1(1, g)
-        load_list()
-        load_list()
-        load_gate()
-        for d in range(3):
-            load_list()
+        load_gate(4, 6)
         for b in (2, 3):
             for g in range(PASSES):
                 load_w1(b, g)
@@ -103,12 +101,16 @@ def tile_picked_gcn_mlp_relu_sub_l_kernel(
         def prepare_w1(c, copies):
             codes = keep.tile([P, PASSES, P], U32, align_bytes=64, name=f"w1_codes{c}")
             scales = keep.tile([P, PASSES, P], U8, align_bytes=64, name=f"w1_scales{c}")
-            steps = []
+            grouped = keep.tile([P, PASSES, P, J], BF16, align_bytes=64, name=f"w1_grouped{c}")
             for g in range(PASSES):
-                grouped = keep.tile([P, P, J], BF16, align_bytes=64, name=f"w1_grouped{c}_{g}")
-                interleave(copies[g], grouped[:], w1_raw[c][g][:])
-                steps.append(lambda g=g, grouped=grouped: quantize(nc, codes[:, g, :], scales[:, g, :], grouped[:]))
-            return codes, scales, steps
+                interleave(copies[g], grouped[:, g], w1_raw[c][g][:])
+            for lo, hi in ((0, 2), (2, 3)):
+                nc.vector.quantize_mx(
+                    out=codes[:, lo:hi, :].rearrange("p g c -> p (g c)").bitcast(FP8X4),
+                    scales=scales[:, lo:hi, :].rearrange("p g c -> p (g c)"),
+                    in_=grouped[:, lo:hi].rearrange("p g c j -> p (g c j)"),
+                )
+            return codes, scales
 
         def project(c, codes, scales, widths):
             h = keep.tile([P, T], F32, name=f"h{c}")
@@ -140,31 +142,31 @@ def tile_picked_gcn_mlp_relu_sub_l_kernel(
             t = keep.tile([P, 2, P, 2], BF16, align_bytes=64, name=f"zt{vh}")
             zt.append(t)
 
-        def gather_sum(c, h, first, count, between):
+        def gather_sum(c, h, last_halves):
             zps = []
-            for vh in range(first, first + count):
+            for vh in range(VH):
                 t = psum_z.tile([P, P], F32, name="zps", tag="zps")
                 zps.append(t)
-            n = count * P
             for d in range(D):
-                prod = prods.tile([P, V], F32, name="prod", tag="prod")
-                nc.vector.tensor_tensor(
-                    prod[:, :n],
-                    h[:].indirect(lists[d][:, first * 8 : (first + count) * 8]),
-                    gate_all[d // 3][:, d % 3, first * P : first * P + n],
-                    MULT,
-                )
-                for i in range(count):
-                    nc.tensor.matmul(
-                        zps[i][:], prod[:, i * P : (i + 1) * P], ident[:],
-                        start=(d == 0), stop=(d == D - 1), is_transpose=True,
+                halves = ((0, 1), (1, 1)) if last_halves and d == D - 1 else ((0, 2),)
+                for first, count in halves:
+                    prod = prods.tile([P, V], F32, name="prod", tag="prod")
+                    nc.vector.tensor_tensor(
+                        prod[:, : count * P],
+                        h[:].indirect(lists[d][:, first * 8 : (first + count) * 8]),
+                        gate_all[d][:, first * P : (first + count) * P],
+                        MULT,
                     )
-                for step in between.get(d, ()):
-                    step()
-            for i in range(count):
-                nc.scalar.copy(
-                    out=zt[first + i][:, :, 32 * c : 32 * c + 32, :],
-                    in_=zps[i][:].rearrange("v (p u e) -> v u p e", u=2, e=2),
+                    for i in range(count):
+                        nc.tensor.matmul(
+                            zps[first + i][:], prod[:, i * P : (i + 1) * P], ident[:],
+                            start=(d == 0), stop=(d == D - 1), is_transpose=True,
+                        )
+            for vh in range(VH):
+                copy = nc.vector.tensor_copy if last_halves and vh == 1 else nc.scalar.copy
+                copy(
+                    out=zt[vh][:, :, 32 * c : 32 * c + 32, :],
+                    in_=zps[vh][:].rearrange("v (p u e) -> v u p e", u=2, e=2),
                 )
 
         w2_grouped = keep.tile([P, N, J], BF16, align_bytes=64)
@@ -172,7 +174,6 @@ def tile_picked_gcn_mlp_relu_sub_l_kernel(
         w2_scales = keep.tile([P, N], U8, align_bytes=64)
         z_codes = keep.tile([P, V], U32, align_bytes=64)
         z_scales = keep.tile([P, V], U8, align_bytes=64)
-        hs = {}
 
         def finish(vh):
             cols = slice(vh * P, (vh + 1) * P)
@@ -181,7 +182,8 @@ def tile_picked_gcn_mlp_relu_sub_l_kernel(
             for u in range(2):
                 nc.tensor.transpose(back[:, u, :], words[:, u * P : (u + 1) * P], ident[:])
             grouped = keep.tile([P, P, J], BF16, align_bytes=64, name=f"z_grouped{vh}")
-            nc.vector.tensor_copy(
+            copy = (nc.scalar.copy, nc.vector.tensor_copy)[vh]
+            copy(
                 out=grouped[:].rearrange("p v j -> p (v j)").bitcast(F32).rearrange("p (v u) -> p v u", u=2),
                 in_=back[:].rearrange("p u v -> p v u"),
             )
@@ -198,7 +200,7 @@ def tile_picked_gcn_mlp_relu_sub_l_kernel(
                     start=True,
                     stop=True,
                 )
-            nc.scalar.copy(out=res[:], in_=ops[:])
+            copy(out=res[:], in_=ops[:])
             nc.sync.dma_start(out=out[:, cols].rearrange("(b p) v -> p b v", p=P), in_=res[:])
 
         x_codes, x_scales = [], []
@@ -208,46 +210,28 @@ def tile_picked_gcn_mlp_relu_sub_l_kernel(
             t = keep.tile([P, T], U8, align_bytes=64, name=f"x_scales{g}")
             x_scales.append(t)
 
-        def prepare_x(g, lo, hi, vector_cols):
-            width = hi - lo
-            grouped = keep.tile([P, width, J], BF16, align_bytes=64, name=f"x_grouped{g}_{lo}")
-            raw = x_raw[g, lo]
-            interleave(nc.vector.tensor_copy, grouped[:, :vector_cols, :], raw[:, :, :vector_cols])
-            interleave(nc.scalar.copy, grouped[:, vector_cols:, :], raw[:, :, vector_cols:])
-            for first, last in ((0, vector_cols), (vector_cols, width)) if width > 256 else ((0, width),):
-                cols = slice(lo + first, lo + last)
-                quantize(nc, x_codes[g][:, cols], x_scales[g][:, cols], grouped[:, first:last, :])
+        def prepare_x(g, vector_cols):
+            grouped = keep.tile([P, T, J], BF16, align_bytes=64, name=f"x_grouped{g}")
+            for lo in range(0, vector_cols, 256):
+                hi = min(lo + 256, vector_cols)
+                interleave(nc.vector.tensor_copy, grouped[:, lo:hi, :], x_raw[g][:, :, lo:hi])
+            interleave(nc.scalar.copy, grouped[:, vector_cols:, :], x_raw[g][:, :, vector_cols:])
+            for lo in (0, 256):
+                cols = slice(lo, lo + 256)
+                quantize(nc, x_codes[g][:, cols], x_scales[g][:, cols], grouped[:, cols, :])
 
         sc, ve = nc.scalar.copy, nc.vector.tensor_copy
-        w1q = {}
-
-        def prepare(c, copies):
-            w1q[c] = prepare_w1(c, copies)
-
-        def q(c, g):
-            w1q[c][2][g]()
-
-        def next_h(c, widths):
-            hs[c] = project(c, w1q[c][0], w1q[c][1], widths)
-
-        prepare(0, (ve, sc, ve))
-        for g in range(PASSES):
-            q(0, g)
-        for g, lo, hi in x_pieces:
-            prepare_x(g, lo, hi, 256 if hi - lo == T else 160)
-        next_h(0, (256, 256))
+        codes, scales = prepare_w1(0, (ve, sc, ve))
+        for g, vector_cols in enumerate((256, 256, 352)):
+            prepare_x(g, vector_cols)
+        hs = [project(0, codes, scales, (256, 256))]
         for c in range(CB):
             if c + 1 < CB:
-                prepare(c + 1, (sc, sc, sc))
-                for g in range(PASSES):
-                    q(c + 1, g)
-                next_h(c + 1, (T,))
+                codes, scales = prepare_w1(c + 1, (sc, sc, sc))
+                hs.append(project(c + 1, codes, scales, (T,)))
             else:
                 interleave(sc, w2_grouped[:], w2_raw[:])
                 quantize(nc, w2_codes[:], w2_scales[:], w2_grouped[:])
-            if c + 1 < CB:
-                gather_sum(c, hs[c], 0, VH, {})
-            else:
-                gather_sum(c, hs[c], 0, 1, {})
-                gather_sum(c, hs[c], 1, 1, {3: [lambda: finish(0)]})
-        finish(1)
+            gather_sum(c, hs[c], c == CB - 1)
+        for vh in range(VH):
+            finish(vh)

from contextlib import ExitStack

import concourse.mybir as mybir
from concourse.masks import make_identity

K, T, D, V, H, N = 1536, 512, 6, 256, 512, 256
FLOPS = 2 * K * H * T + 2 * H * N * V

F32 = mybir.dt.float32
BF16 = mybir.dt.bfloat16
U32 = mybir.dt.uint32
U16 = mybir.dt.uint16
U8 = mybir.dt.uint8
FP8X4 = mybir.dt.float8_e4m3fn_x4
RELU = mybir.ActivationFunctionType.Relu
MULT = mybir.AluOpType.mult

P = 128
J = 4
KP = P * J
PASSES = K // KP
CB = H // P
VH = V // P


def interleave(copy, grouped, raw):
    copy(
        out=grouped.rearrange("p (c i) j -> p c j i", i=4),
        in_=raw.rearrange("p j (c i) -> p c j i", i=4),
    )


def quantize(nc, codes, scales, grouped):
    nc.vector.quantize_mx(
        out=codes.bitcast(FP8X4), scales=scales, in_=grouped.rearrange("p c j -> p (c j)")
    )


def tile_picked_gcn_mlp_relu_sub_l_kernel(
    tc, xT, w1, w2, gate, pos1, pos2, pos3, pos4, pos5, pos6, out
):
    nc = tc.nc
    with ExitStack() as ctx:
        keep = ctx.enter_context(tc.tile_pool(name="keep", bufs=1))
        prods = ctx.enter_context(tc.tile_pool(name="prods", bufs=12))
        psum_h = ctx.enter_context(tc.psum_pool(name="psum_h", bufs=2))
        psum_z = ctx.enter_context(tc.psum_pool(name="psum_z", bufs=4))
        psum_m = ctx.enter_context(tc.psum_pool(name="psum_m", bufs=2))

        gate_all = []

        def load_gate(first, last):
            t = keep.tile([P, last - first, V], F32, name=f"gate{first}")
            nc.sync.dma_start(out=t[:], in_=gate[first:last].rearrange("d p v -> p d v"))
            for i in range(last - first):
                gate_all.append(t[:, i, :])

        w1_raw = [[], [], [], []]

        def load_w1(b, g):
            t = keep.tile([P, J, P], F32, name=f"w1_raw{b}_{g}")
            nc.sync.dma_start(out=t[:], in_=w1[g * KP : (g + 1) * KP, b * P : (b + 1) * P].rearrange("(p j) c -> p j c", j=J))
            w1_raw[b].append(t)

        x_raw = []

        def load_x(g):
            t = keep.tile([P, J, T], F32, name=f"x_raw{g}")
            nc.sync.dma_start(out=t[:], in_=xT[g * KP : (g + 1) * KP, :].rearrange("(p j) t -> p j t", j=J))
            x_raw.append(t)

        lists = []

        def load_list():
            d = len(lists)
            t = keep.tile([P, V // 16], U16, name=f"list{d}")
            nc.sync.dma_start(t[:], (pos1, pos2, pos3, pos4, pos5, pos6)[d])
            lists.append(t)

        for g in range(PASSES):
            load_w1(0, g)
        load_list()
        load_list()
        for g in range(PASSES):
            load_x(g)
        for d in range(4):
            load_list()
        load_gate(0, 4)
        for g in range(PASSES):
            load_w1(1, g)
        load_gate(4, 6)
        for b in (2, 3):
            for g in range(PASSES):
                load_w1(b, g)
        w2_raw = keep.tile([P, J, N], F32)
        nc.sync.dma_start(out=w2_raw[:], in_=w2.rearrange("(p j) m -> p j m", j=J))

        ident = keep.tile([P, P], F32)
        make_identity(nc, ident[:])

        def prepare_w1(c, copies):
            codes = keep.tile([P, PASSES, P], U32, align_bytes=64, name=f"w1_codes{c}")
            scales = keep.tile([P, PASSES, P], U8, align_bytes=64, name=f"w1_scales{c}")
            grouped = keep.tile([P, PASSES, P, J], BF16, align_bytes=64, name=f"w1_grouped{c}")
            for g in range(PASSES):
                interleave(copies[g], grouped[:, g], w1_raw[c][g][:])
            for lo, hi in ((0, 2), (2, 3)):
                nc.vector.quantize_mx(
                    out=codes[:, lo:hi, :].rearrange("p g c -> p (g c)").bitcast(FP8X4),
                    scales=scales[:, lo:hi, :].rearrange("p g c -> p (g c)"),
                    in_=grouped[:, lo:hi].rearrange("p g c j -> p (g c j)"),
                )
            return codes, scales

        def project(c, codes, scales, widths):
            h = keep.tile([P, T], F32, name=f"h{c}")
            parts, lo = [], 0
            for n in widths:
                hp = psum_h.tile([P, T], F32, name="hp", tag="hp")
                parts.append((hp, n, slice(lo, lo + n)))
                lo += n
            for g in range(PASSES):
                for hp, n, cols in parts:
                    nc.tensor.matmul_mx(
                        out=hp[:, :n],
                        lhsT=codes[:, g, :].bitcast(FP8X4),
                        lhsT_scale=scales[:, g, :],
                        rhs=x_codes[g][:, cols].bitcast(FP8X4),
                        rhs_scale=x_scales[g][:, cols],
                        start=(g == 0),
                        stop=(g == PASSES - 1),
                    )
            for i, (hp, n, cols) in enumerate(parts):
                if i == 0:
                    nc.scalar.activation(out=h[:, cols], in_=hp[:, :n], func=RELU)
                else:
                    nc.vector.tensor_relu(out=h[:, cols], in_=hp[:, :n])
            return h

        zt = []
        for vh in range(VH):
            t = keep.tile([P, 2, P, 2], BF16, align_bytes=64, name=f"zt{vh}")
            zt.append(t)

        def gather_sum(c, h, last_halves):
            zps = []
            for vh in range(VH):
                t = psum_z.tile([P, P], F32, name="zps", tag="zps")
                zps.append(t)
            for d in range(D):
                halves = ((0, 1), (1, 1)) if last_halves and d == D - 1 else ((0, 2),)
                for first, count in halves:
                    prod = prods.tile([P, V], F32, name="prod", tag="prod")
                    nc.vector.tensor_tensor(
                        prod[:, : count * P],
                        h[:].indirect(lists[d][:, first * 8 : (first + count) * 8]),
                        gate_all[d][:, first * P : (first + count) * P],
                        MULT,
                    )
                    for i in range(count):
                        nc.tensor.matmul(
                            zps[first + i][:], prod[:, i * P : (i + 1) * P], ident[:],
                            start=(d == 0), stop=(d == D - 1), is_transpose=True,
                        )
            for vh in range(VH):
                copy = nc.vector.tensor_copy if last_halves and vh == 1 else nc.scalar.copy
                copy(
                    out=zt[vh][:, :, 32 * c : 32 * c + 32, :],
                    in_=zps[vh][:].rearrange("v (p u e) -> v u p e", u=2, e=2),
                )

        w2_grouped = keep.tile([P, N, J], BF16, align_bytes=64)
        w2_codes = keep.tile([P, N], U32, align_bytes=64)
        w2_scales = keep.tile([P, N], U8, align_bytes=64)
        z_codes = keep.tile([P, V], U32, align_bytes=64)
        z_scales = keep.tile([P, V], U8, align_bytes=64)

        def finish(vh):
            cols = slice(vh * P, (vh + 1) * P)
            words = zt[vh][:].rearrange("v u p e -> v (u p e)").bitcast(F32)
            back = psum_m.tile([P, 2, P], F32, name="back", tag="m")
            for u in range(2):
                nc.tensor.transpose(back[:, u, :], words[:, u * P : (u + 1) * P], ident[:])
            grouped = keep.tile([P, P, J], BF16, align_bytes=64, name=f"z_grouped{vh}")
            copy = (nc.scalar.copy, nc.vector.tensor_copy)[vh]
            copy(
                out=grouped[:].rearrange("p v j -> p (v j)").bitcast(F32).rearrange("p (v u) -> p v u", u=2),
                in_=back[:].rearrange("p u v -> p v u"),
            )
            quantize(nc, z_codes[:, cols], z_scales[:, cols], grouped[:])
            res = keep.tile([P, 2, P], F32, name=f"res{vh}")
            ops = psum_h.tile([P, 2, P], F32, name="ops", tag="hp")
            for mb in range(N // P):
                nc.tensor.matmul_mx(
                    out=ops[:, mb, :],
                    lhsT=w2_codes[:, mb * P : (mb + 1) * P].bitcast(FP8X4),
                    lhsT_scale=w2_scales[:, mb * P : (mb + 1) * P],
                    rhs=z_codes[:, cols].bitcast(FP8X4),
                    rhs_scale=z_scales[:, cols],
                    start=True,
                    stop=True,
                )
            copy(out=res[:], in_=ops[:])
            nc.sync.dma_start(out=out[:, cols].rearrange("(b p) v -> p b v", p=P), in_=res[:])

        x_codes, x_scales = [], []
        for g in range(PASSES):
            t = keep.tile([P, T], U32, align_bytes=64, name=f"x_codes{g}")
            x_codes.append(t)
            t = keep.tile([P, T], U8, align_bytes=64, name=f"x_scales{g}")
            x_scales.append(t)

        def prepare_x(g, vector_cols):
            grouped = keep.tile([P, T, J], BF16, align_bytes=64, name=f"x_grouped{g}")
            for lo in range(0, vector_cols, 256):
                hi = min(lo + 256, vector_cols)
                interleave(nc.vector.tensor_copy, grouped[:, lo:hi, :], x_raw[g][:, :, lo:hi])
            interleave(nc.scalar.copy, grouped[:, vector_cols:, :], x_raw[g][:, :, vector_cols:])
            for lo in (0, 256):
                cols = slice(lo, lo + 256)
                quantize(nc, x_codes[g][:, cols], x_scales[g][:, cols], grouped[:, cols, :])

        sc, ve = nc.scalar.copy, nc.vector.tensor_copy
        codes, scales = prepare_w1(0, (ve, sc, ve))
        for g, vector_cols in enumerate((256, 256, 352)):
            prepare_x(g, vector_cols)
        hs = [project(0, codes, scales, (256, 256))]
        for c in range(CB):
            if c + 1 < CB:
                codes, scales = prepare_w1(c + 1, (sc, sc, sc))
                hs.append(project(c + 1, codes, scales, (T,)))
            else:
                interleave(sc, w2_grouped[:], w2_raw[:])
                quantize(nc, w2_codes[:], w2_scales[:], w2_grouped[:])
            gather_sum(c, hs[c], c == CB - 1)
        for vh in range(VH):
            finish(vh)
